import numpy as np
import ml_dtypes


def mxq(x, axis, fmt="e4m3"):
    dtype, down = {"e4m3": (ml_dtypes.float8_e4m3fn, 7), "e5m2": (ml_dtypes.float8_e5m2, 14)}[fmt]
    v = np.moveaxis(np.asarray(x, np.float32).astype(ml_dtypes.bfloat16).astype(np.float64), axis, -1)
    blocks = v.reshape(v.shape[:-1] + (-1, 32))
    amax = np.abs(blocks).max(-1, keepdims=True)
    byte = np.maximum(np.where(amax > 0, np.frexp(amax)[1] - 1 + 127, 0) - down, 1)
    scale = np.exp2(byte - 127.0)
    codes = (blocks / scale).astype(np.float32).astype(dtype).astype(np.float64)
    return np.moveaxis((codes * scale).reshape(v.shape), -1, axis)


WIDE = False


def mx_kscale(k):
    if not WIDE:
        return np.ones(k)
    levels = np.array([10, -10, 5, -5, 0])
    if k % 512:
        return np.exp2(np.random.permutation(np.resize(levels, k // 32))).repeat(32)
    a = np.empty((k // 512, 16))
    for p in range(k // 512):
        a[p, :8] = np.random.permutation(np.resize(levels, 8))
        for g in range(8):
            far = levels[np.abs(levels - a[p, g]) >= 10]
            a[p, g + 8] = far[np.random.randint(len(far))]
    return np.exp2(a.ravel()).repeat(32)


def f64(x):
    return np.asarray(x).astype(np.float64)


def striped(idx):
    return np.tile(np.asarray(idx).reshape(-1, 16).T, (8, 1)).astype(np.uint16)


def unstriped(offs):
    return offs[:16].T.reshape(-1).astype(np.int64)


E2M1 = np.array([0.0, 0.5, 1.0, 1.5, 2.0, 3.0, 4.0, 6.0, -0.0, -0.5, -1.0, -1.5, -2.0, -3.0, -4.0, -6.0])


def pack_weight(w, fmt):
    k, n = w.shape
    w = f64(np.asarray(w, np.float32).astype(ml_dtypes.bfloat16)).reshape(k // 32, 32, n)
    amax = np.abs(w).max(1)
    if fmt == "e4m3":
        byte = np.frexp(amax)[1] - 1 + 127 - 7
    else:
        mant, ex = np.frexp(amax / 6.0)
        byte = np.where(mant > 0.5, ex, ex - 1) + 127
    byte = np.clip(np.where(amax > 0, byte, 1), 1, 254)
    scaled = (w * np.exp2(127.0 - byte)[:, None, :]).reshape(k, n).astype(np.float32)
    by_word = np.ascontiguousarray(scaled.reshape(k // 512, 128, 4, n).transpose(0, 1, 3, 2))
    if fmt == "e4m3":
        words = by_word.astype(ml_dtypes.float8_e4m3fn).view(np.uint8)
    else:
        c = by_word.astype(ml_dtypes.float4_e2m1fn).view(np.uint8) & 0xF
        words = (c[..., 0::2] | (c[..., 1::2] << 4)).reshape(k // 512, 128, 2 * n)
    return np.ascontiguousarray(words), np.ascontiguousarray(byte.astype(np.uint8).reshape(k // 512, 16, n))


def unpack_weight(words, scales, fmt):
    g, _, n = scales.shape
    words = np.ascontiguousarray(words).reshape(g, 128, n, -1)
    if fmt == "e4m3":
        vals = words.view(ml_dtypes.float8_e4m3fn).astype(np.float64)
    else:
        nib = np.empty((g, 128, n, 4), np.uint8)
        nib[..., 0::2] = words & 0xF
        nib[..., 1::2] = words >> 4
        vals = E2M1[nib]
    vals = vals * np.repeat(np.exp2(scales.astype(np.float64) - 127.0), 8, axis=1)[..., None]
    return vals.transpose(0, 1, 3, 2).reshape(g * 512, n)


def sigmoid(v):
    return 1.0 / (1.0 + np.exp(-v))


def bf(x):
    return np.asarray(x, np.float32).astype(ml_dtypes.bfloat16)


def planes(Y):
    r, m = Y.shape
    b = f64(bf(Y)).reshape(r // 32, 32, m)
    amax = np.abs(b).max(1)
    byte = np.clip(np.where(amax > 0, np.frexp(amax)[1] - 1 + 127 - 7, 1), 1, 254)
    codes = (b * np.exp2(127.0 - byte)[:, None, :]).reshape(r, m).astype(np.float32).astype(ml_dtypes.float8_e4m3fn).view(np.uint8)
    words = codes.reshape(r // 512, 128, 4, m).transpose(0, 1, 3, 2)
    return np.ascontiguousarray(words), np.ascontiguousarray(byte.astype(np.uint8).reshape(r // 512, 16, m))


D, T, I, Q, E, V = 512, 2048, 512, 256, 512, 32


def setup_inputs():
    n = np.random.standard_normal
    idx = np.random.permutation(T)[:I]
    fd = mx_kscale(D)
    fi = mx_kscale(I)
    ti = np.ones(T)
    ti[idx] = fi
    keysp = pack_weight(n((D, T)) / fd[:, None], "e2m1")
    return {
        "query": (n((D, Q)) * 1.0 / np.sqrt(D) * fd[:, None]).astype(np.float32),
        "keys_words": keysp[0],
        "keys_scales": keysp[1],
        "lam": (np.random.uniform(0.3, 0.8, (1, Q))).astype(np.float32),
        "eager": (np.random.uniform(0.8, 2.0, (Q, 1))).astype(np.float32),
        "thresh": (np.random.uniform(1.5, 4.0, (Q, 1))).astype(np.float32),
        "os": (np.random.uniform(4.0, 16.0, (1, I)) * fi).astype(np.float32),
        "vals": (n((E, T)) / ti).astype(np.float32),
        "memq": (np.random.uniform(0.3, 1.0, (1, Q))).astype(np.float32),
        "offs": striped(idx),
    }


def reference(query, keys_words, keys_scales, lam, eager, thresh, os, vals, memq, offs):
    idx = unstriped(offs)
    keysu = unpack_weight(keys_words, keys_scales, "e2m1")
    keysidxg = keysu[:, idx]
    queryq = mxq(f64(query), 0, "e4m3")
    a0 = keysidxg.T @ queryq
    ag = a0.reshape(I, V, Q // V).max(axis=2)
    ar = np.repeat(ag, Q // V, axis=1)
    s0 = a0 - ar * f64(lam)
    s = s0.T
    m0 = np.max(s, axis=1, keepdims=True)
    m1 = np.mean(s, axis=1, keepdims=True)
    p = np.exp(s - m0)
    gt0 = sigmoid((m0 - m1) * f64(eager) - f64(thresh))
    w = p / np.sum(p, axis=1, keepdims=True) * gt0
    wo1 = w * f64(os)
    wt1 = wo1.T
    vt1 = f64(vals)[:, idx].T
    vt1q = mxq(vt1, 0, "e4m3")
    wt1q = mxq(wt1, 0, "e4m3")
    o = vt1q.T @ wt1q
    o1 = np.pad(o, ((0, 0), (1, 0)))[:, :Q]
    y = o - o1 * f64(memq)
    words, scales = planes(y)
    return y, words, scales

@@ -1,0 +1,265 @@
+from contextlib import ExitStack
+
+import concourse.mybir as mybir
+from concourse.masks import make_identity
+
+D, T, I, Q, E, V = 512, 2048, 512, 256, 512, 32
+FLOPS = 2 * D * I * Q + 2 * I * E * Q
+
+F32 = mybir.dt.float32
+BF16 = mybir.dt.bfloat16
+I32 = mybir.dt.int32
+U32 = mybir.dt.uint32
+U16 = mybir.dt.uint16
+U8 = mybir.dt.uint8
+FP8X4 = mybir.dt.float8_e4m3fn_x4
+FP4X4 = mybir.dt.float4_e2m1fn_x4
+ALU = mybir.AluOpType
+ACT = mybir.ActivationFunctionType
+AX = mybir.AxisListType
+
+P = 128
+PACK = 4
+GROUP = Q // V
+HALVES = Q // P
+
+
+def tile_attend_groupbest_abstaining_rowchanges_pl_kernel(
+    tc, query, keys_words, keys_scales, lam, eager, thresh, slot_factor, vals, memq, offs, out_0, out_1, out_2
+):
+    nc = tc.nc
+    with ExitStack() as ctx:
+        sb = ctx.enter_context(tc.tile_pool(name="sb", bufs=1))
+        ps = ctx.enter_context(tc.psum_pool(name="ps", bufs=1))
+
+        def bank(shape, number, name):
+            return ps.tile(shape, F32, name=name, tag="bank%d" % number)
+
+        offsets = sb.tile([P, I // 16], U16, name="offsets")
+        nc.sync.dma_start(offsets[:], offs)
+        key_scale_pool = sb.tile([P, T], U8, name="key_scale_pool", align_bytes=64)
+        nc.vector.memset(key_scale_pool[:].bitcast(I32), 0)
+        query_raw = sb.tile([P, PACK, Q], F32, name="query_raw")
+        nc.sync.dma_start(query_raw[:], query.rearrange("(p t) q -> p t q", t=PACK))
+        for quad in range(4):
+            nc.sync.dma_start(
+                key_scale_pool[32 * quad : 32 * quad + 4, :].bitcast(I32),
+                keys_scales[0, 4 * quad : 4 * quad + 4, :].bitcast(I32),
+            )
+        key_word_pool = sb.tile([P, T], U16, name="key_word_pool", align_bytes=64)
+        nc.sync.dma_start(key_word_pool[:].bitcast(I32), keys_words[0].bitcast(I32))
+
+        vals_planes = vals.rearrange("(p t) c -> t p c", t=PACK)
+        val_pool = [sb.tile([P, T], F32, name="val_pool%d" % t, tag="val_pool%d" % t, align_bytes=64) for t in range(PACK)]
+        nc.sync.dma_start(val_pool[0][:], vals_planes[0])
+
+        lam_col = sb.tile([P, HALVES], F32, name="lam_col", tag="lam_col", align_bytes=64)
+        nc.sync.dma_start(lam_col[:], lam.rearrange("o (p a) -> p (o a)", a=HALVES))
+        os_col = sb.tile([P, PACK], F32, name="os_col")
+        nc.sync.dma_start(os_col[:], slot_factor.rearrange("o (p m) -> p (o m)", m=PACK))
+        memq_col = sb.tile([P, HALVES], F32, name="memq_col")
+        nc.sync.dma_start(memq_col[:], memq.rearrange("o (p a) -> p (o a)", a=HALVES))
+        eager_col = sb.tile([P, HALVES], F32, name="eager_col")
+        nc.sync.dma_start(eager_col[:], eager.rearrange("(p a) o -> p (a o)", a=HALVES))
+        thresh_col = sb.tile([P, HALVES], F32, name="thresh_col")
+        nc.sync.dma_start(thresh_col[:], thresh.rearrange("(p a) o -> p (a o)", a=HALVES))
+        for t in range(1, PACK):
+            nc.sync.dma_start(val_pool[t][:], vals_planes[t])
+
+        ident = sb.tile([P, P], F32, name="ident")
+        make_identity(nc, ident[:])
+
+        query_bf = sb.tile([P, Q, PACK], BF16, name="query_bf", tag="query_bf", align_bytes=64)
+        nc.scalar.activation(
+            query_bf[:].rearrange("p (c i) t -> p c t i", i=4),
+            query_raw[:].rearrange("p t (c i) -> p c t i", i=4),
+            ACT.Copy,
+        )
+        key_scales = sb.tile([P, I], U8, name="key_scales", align_bytes=64)
+        nc.vector.tensor_copy(key_scales[:], key_scale_pool[:].indirect(offsets[:]))
+        half = I // 32
+        key_words = [sb.tile([P, I // 2], U16, name="key_words0", align_bytes=64)]
+        nc.vector.tensor_copy(key_words[0][:], key_word_pool[:].indirect(offsets[:, 0:half]))
+        query_codes = sb.tile([P, Q], U32, name="query_codes", align_bytes=64)
+        query_scales = sb.tile([P, Q], U8, name="query_scales", align_bytes=64)
+        nc.vector.quantize_mx(
+            out=query_codes[:].bitcast(FP8X4), scales=query_scales[:], in_=query_bf[:].rearrange("p q t -> p (q t)")
+        )
+
+        key_words.append(sb.tile([P, I // 2], U16, name="key_words1", tag="query_bf", align_bytes=64))
+        nc.vector.tensor_copy(key_words[1][:], key_word_pool[:].indirect(offsets[:, half : 2 * half]))
+        raw_ps = [bank([P, 2, Q], h, "raw_ps%d" % h) for h in range(2)]
+        for r in range(4):
+            cols = slice(r * P, (r + 1) * P)
+            nc.tensor.matmul_mx(
+                out=raw_ps[r // 2][:, r % 2, :],
+                lhsT=key_words[r // 2][:, (r % 2) * P : (r % 2 + 1) * P].bitcast(FP4X4),
+                lhsT_scale=key_scales[:, cols],
+                rhs=query_codes[:].bitcast(FP8X4),
+                rhs_scale=query_scales[:],
+                start=True,
+                stop=True,
+            )
+
+        best = [sb.tile([P, 2 * V, 1], F32, name="best%d" % h) for h in range(2)]
+        best_rep = [sb.tile([P, 2 * V, P // V], F32, name="best_rep%d" % h) for h in range(2)]
+        raw_sb = [sb.tile([P, 2, HALVES, P], F32, name="raw_sb%d" % h) for h in range(2)]
+        for h in range(2):
+            nc.vector.tensor_reduce(
+                best[h][:, :, 0],
+                raw_ps[h][:].rearrange("p r (v j) -> p (r v) j", j=GROUP),
+                AX.X,
+                ALU.max,
+            )
+            nc.scalar.copy(raw_sb[h][:], raw_ps[h][:].rearrange("p r (m a) -> p r a m", a=HALVES))
+        for h in range(2):
+            nc.vector.tensor_copy(best_rep[h][:], best[h][:].to_broadcast([P, 2 * V, P // V]))
+        best_t = sb.tile([P, I], F32, name="best_t", tag="best_t", align_bytes=64)
+        raw_t_ps = [bank([P, 4, P], 2 + a, "raw_t_ps%d" % a) for a in range(HALVES)]
+        for h in range(2):
+            best_ps = bank([P, 2, P], 4 + 2 * h, "best_ps%d" % h)
+            for r in range(2):
+                nc.tensor.transpose(
+                    best_ps[:, r, :], best_rep[h][:, V * r : V * (r + 1), :].rearrange("p v j -> p (v j)"), ident[:]
+                )
+            nc.scalar.copy(best_t[:, 2 * P * h : 2 * P * (h + 1)], best_ps[:].rearrange("p r m -> p (r m)"))
+        for a in range(HALVES):
+            for r in range(4):
+                nc.tensor.transpose(raw_t_ps[a][:, r, :], raw_sb[r // 2][:, r % 2, a, :], ident[:])
+
+        val_codes = [sb.tile([P, P], U32, name="val_codes%d" % t, align_bytes=64) for t in range(PACK)]
+        val_scales = [sb.tile([P, P], U8, name="val_scales%d" % t, align_bytes=64) for t in range(PACK)]
+        val_bf = []
+
+        def gather_vals(t):
+            picked = sb.tile([P, I], BF16, name="picked%d" % t, tag=("picked0", "best_t", "lam_col", "p1")[t], align_bytes=64)
+            nc.vector.tensor_copy(picked[:], val_pool[t][:].indirect(offsets[:]))
+            pairs = picked[:].bitcast(F32)
+            turned = bank([P, 2, P], (6, 7, 6, 4)[t], "val_turned%d" % t)
+            for u in range(2):
+                nc.tensor.transpose(turned[:, u, :], pairs[:, u : 2 * P : 2], ident[:])
+            return turned
+
+        def weave_vals(t, turned):
+            val_bf.append(
+                sb.tile([P, P, PACK], BF16, name="val_bf%d" % t, tag=("val_bf0", "odds", "p_sum", "val_bf3")[t], align_bytes=64)
+            )
+            nc.scalar.copy(
+                val_bf[t][:].rearrange("p e t -> p (e t)").bitcast(F32).rearrange("p (e u) -> p e u", u=2),
+                turned[:].rearrange("p u e -> p e u"),
+            )
+
+        def quantize_vals(t):
+            nc.vector.quantize_mx(
+                out=val_codes[t][:].bitcast(FP8X4), scales=val_scales[t][:], in_=val_bf[t][:].rearrange("p e t -> p (e t)")
+            )
+
+        weave_vals(0, gather_vals(0))
+
+        os_ps = bank([P, PACK, P], 5, "os_ps")
+        for m in range(PACK):
+            nc.tensor.transpose(os_ps[:, m, :], os_col[:, m : m + 1].to_broadcast([P, P]), ident[:])
+        memq_ps = bank([P, HALVES, P], 7, "memq_ps")
+        for a in range(HALVES):
+            nc.tensor.transpose(memq_ps[:, a, :], memq_col[:, a : a + 1].to_broadcast([P, P]), ident[:])
+        memq_row = sb.tile([P, 1, Q], F32, name="memq_row")
+        nc.scalar.copy(memq_row[:, 0, :].rearrange("p (m a) -> p m a", a=HALVES), memq_ps[:].rearrange("p a m -> p m a"))
+
+        neg_both = sb.tile([P, HALVES * I], F32, name="neg_both", tag="val_pool0", align_bytes=64)
+        neg_s = [neg_both[:, a * I : (a + 1) * I] for a in range(HALVES)]
+        neg_sum = sb.tile([P, HALVES], F32, name="neg_sum")
+        neg_max = sb.tile([P, HALVES], F32, name="neg_max")
+        gap = sb.tile([P, HALVES], F32, name="gap")
+        p_sum = sb.tile([P, HALVES], F32, name="p_sum", tag="p_sum", align_bytes=64)
+        odds = sb.tile([P, HALVES], F32, name="odds", tag="odds", align_bytes=64)
+        denom = sb.tile([P, HALVES], F32, name="denom")
+        p = [sb.tile([P, I], F32, name="p%d" % a, tag="p%d" % a, align_bytes=64) for a in range(HALVES)]
+        for a in range(HALVES):
+            nc.vector.scalar_tensor_tensor(
+                neg_s[a], best_t[:], lam_col[:, a : a + 1], raw_t_ps[a][:].rearrange("p r m -> p (r m)"),
+                ALU.mult, ALU.subtract, accum_out=neg_sum[:, a : a + 1],
+            )
+        for a in range(HALVES):
+            col = slice(a, a + 1)
+            nc.vector.tensor_reduce(neg_max[:, col], neg_s[a], AX.X, ALU.min)
+            nc.scalar.activation(p[a][:], neg_s[a], ACT.Exp, bias=neg_max[:, col], scale=-1.0, accum_out=p_sum[:, col])
+            nc.gpsimd.tensor_scalar(gap[:, col], neg_sum[:, col], -1.0 / I, neg_max[:, col], ALU.mult, ALU.add)
+        for a in range(HALVES):
+            col = slice(a, a + 1)
+            nc.scalar.activation(odds[:, col], gap[:, col], ACT.Exp, bias=thresh_col[:, col], scale=eager_col[:, col])
+        for a in range(HALVES):
+            col = slice(a, a + 1)
+            nc.scalar.activation(denom[:, col], odds[:, col], ACT.Identity, bias=p_sum[:, col], scale=p_sum[:, col])
+        weave_vals(1, gather_vals(1))
+        quantize_vals(0)
+        weave_vals(2, gather_vals(2))
+        factor = sb.tile([P, HALVES], F32, name="factor", tag="val_pool2", align_bytes=64)
+        nc.vector.reciprocal(factor[:], denom[:])
+
+        w_bf = [sb.tile([P, I], BF16, name="w_bf%d" % a, align_bytes=64) for a in range(HALVES)]
+        w_ps = bank([P, 2, HALVES, P], 4, "w_ps")
+        for a in range(HALVES):
+            nc.vector.scalar_tensor_tensor(
+                w_bf[a][:].rearrange("p (n m) -> p n m", m=PACK),
+                p[a][:].rearrange("p (n m) -> p n m", m=PACK),
+                factor[:, a : a + 1],
+                os_ps[:].rearrange("p m n -> p n m"),
+                ALU.mult, ALU.mult,
+            )
+            pairs = w_bf[a][:].bitcast(F32)
+            for u in range(2):
+                nc.tensor.transpose(w_ps[:, u, a, :], pairs[:, u : 2 * P : 2], ident[:])
+        w_t = sb.tile([P, Q * PACK], BF16, name="w_t", align_bytes=64)
+        nc.scalar.copy(
+            w_t[:].bitcast(F32).rearrange("p (m a u) -> p m a u", a=HALVES, u=2),
+            w_ps[:].rearrange("p u a m -> p m a u"),
+        )
+        quantize_vals(1)
+        weave_vals(3, gather_vals(3))
+        quantize_vals(2)
+        w_codes = sb.tile([P, Q], U32, name="w_codes", tag="val_pool3", align_bytes=64)
+        w_scales = sb.tile([P, Q], U8, name="w_scales", align_bytes=64)
+        nc.vector.quantize_mx(out=w_codes[:].bitcast(FP8X4), scales=w_scales[:], in_=w_t[:])
+        quantize_vals(3)
+
+        o_ps = [bank([P, 2, Q], h, "o_ps%d" % h) for h in range(2)]
+        for t in range(PACK):
+            nc.tensor.matmul_mx(
+                out=o_ps[t // 2][:, t % 2, :],
+                lhsT=val_codes[t][:].bitcast(FP8X4),
+                lhsT_scale=val_scales[t][:],
+                rhs=w_codes[:].bitcast(FP8X4),
+                rhs_scale=w_scales[:],
+                start=True,
+                stop=True,
+            )
+        carried = [sb.tile([P, 2, Q], F32, name="carried%d" % h) for h in range(2)]
+        y = sb.tile([P, PACK, Q], F32, name="y")
+        out_rows = out_0.rearrange("(p t) q -> p t q", t=PACK)
+        for h in range(2):
+            nc.vector.memset(carried[h][:, :, 0:1], 0.0)
+        for h in range(2):
+            nc.vector.tensor_tensor(
+                carried[h][:, :, 1:Q], o_ps[h][:, :, 0 : Q - 1],
+                memq_row[:, :, 1:Q].to_broadcast([P, 2, Q - 1]), ALU.mult,
+            )
+        for h in range(2):
+            nc.vector.tensor_tensor(y[:, 2 * h : 2 * h + 2, :], o_ps[h][:], carried[h][:], ALU.subtract)
+            nc.sync.dma_start(out_rows[:, 2 * h : 2 * h + 2, :], y[:, 2 * h : 2 * h + 2, :])
+
+        y_codes = sb.tile([P, Q], U32, name="y_codes", align_bytes=64)
+        y_scales = sb.tile([P, Q], U8, name="y_scales", align_bytes=64)
+        y_bf = sb.tile([P, Q, PACK], BF16, name="y_bf", align_bytes=64)
+        nc.vector.tensor_copy(
+            y_bf[:].rearrange("p (c i) t -> p c t i", i=4), y[:].rearrange("p t (c i) -> p c t i", i=4)
+        )
+        nc.vector.quantize_mx(
+            out=y_codes[:].bitcast(FP8X4), scales=y_scales[:], in_=y_bf[:].rearrange("p q t -> p (q t)")
+        )
+        nc.sync.dma_start(out_1[0].rearrange("p c r -> p (c r)").bitcast(I32), y_codes[:].bitcast(I32))
+        for quad in range(4):
+            queue = nc.scalar if quad % 2 == 0 else nc.sync
+            queue.dma_start(
+                out_2[0, 4 * quad : 4 * quad + 4, :].bitcast(I32),
+                y_scales[32 * quad : 32 * quad + 4, :].bitcast(I32),
+            )

@@ -20,8 +20,13 @@ AX = mybir.AxisListType
 
 P = 128
 PACK = 4
+QUADS = 4
 GROUP = Q // V
-HALVES = Q // P
+PARITIES = Q // P
+SLOT_TILES = I // P
+LIST_COLS = I // 16
+SCALAR_PLANE = 2
+RUN = 4
 
 
 def tile_attend_groupbest_abstaining_rowchanges_pl_kernel(
@@ -32,232 +37,251 @@ def tile_attend_groupbest_abstaining_rowchanges_pl_kernel(
         sb = ctx.enter_context(tc.tile_pool(name="sb", bufs=1))
         ps = ctx.enter_context(tc.psum_pool(name="ps", bufs=1))
 
+        def tile(shape, dtype, name, after=None):
+            return sb.tile(shape, dtype, name=name, tag=after or name, align_bytes=64)
+
         def bank(shape, number, name):
             return ps.tile(shape, F32, name=name, tag="bank%d" % number)
 
-        offsets = sb.tile([P, I // 16], U16, name="offsets")
+        def load_dealt(vector, width, name):
+            pattern = "o (m c) -> m (o c)" if vector.shape[0] == 1 else "(m c) o -> m (c o)"
+            col = tile([P, width], F32, name)
+            nc.sync.dma_start(col[:], vector.rearrange(pattern, c=width))
+            return col
+
+        def weave_views(woven, rows):
+            return woven.rearrange("p (c i) t -> p c t i", i=RUN), rows.rearrange("p t (c i) -> p c t i", i=RUN)
+
+        def quantize(codes, scales, woven):
+            nc.vector.quantize_mx(out=codes.bitcast(FP8X4), scales=scales, in_=woven)
+
+        def turn_pairs(turned, values):
+            pairs = values.bitcast(F32)
+            for u in range(2):
+                nc.tensor.transpose(turned[:, u, :], pairs[:, u : I // 2 : 2], ident[:])
+
+        offsets = sb.tile([P, LIST_COLS], U16, name="offsets")
         nc.sync.dma_start(offsets[:], offs)
-        key_scale_pool = sb.tile([P, T], U8, name="key_scale_pool", align_bytes=64)
+        key_scale_pool = tile([P, T], U8, "key_scale_pool")
         nc.vector.memset(key_scale_pool[:].bitcast(I32), 0)
-        query_raw = sb.tile([P, PACK, Q], F32, name="query_raw")
+        query_raw = tile([P, PACK, Q], F32, "query_raw")
         nc.sync.dma_start(query_raw[:], query.rearrange("(p t) q -> p t q", t=PACK))
-        for quad in range(4):
+        for quad in range(QUADS):
             nc.sync.dma_start(
                 key_scale_pool[32 * quad : 32 * quad + 4, :].bitcast(I32),
                 keys_scales[0, 4 * quad : 4 * quad + 4, :].bitcast(I32),
             )
-        key_word_pool = sb.tile([P, T], U16, name="key_word_pool", align_bytes=64)
+        key_word_pool = tile([P, T], U16, "key_word_pool")
         nc.sync.dma_start(key_word_pool[:].bitcast(I32), keys_words[0].bitcast(I32))
 
-        vals_planes = vals.rearrange("(p t) c -> t p c", t=PACK)
-        val_pool = [sb.tile([P, T], F32, name="val_pool%d" % t, tag="val_pool%d" % t, align_bytes=64) for t in range(PACK)]
+        vals_planes = vals.rearrange("(m t) c -> t m c", t=PACK)
+        val_pool = [tile([P, T], F32, "val_pool%d" % t) for t in range(PACK)]
         nc.sync.dma_start(val_pool[0][:], vals_planes[0])
+        lam_col = load_dealt(lam, PARITIES, "lam_col")
+        nc.sync.dma_start(val_pool[SCALAR_PLANE][:], vals_planes[SCALAR_PLANE])
+        nc.sync.dma_start(val_pool[1][:], vals_planes[1])
+        eager_col = load_dealt(eager, PARITIES, "eager_col")
+        thresh_col = load_dealt(thresh, PARITIES, "thresh_col")
+        os_col = load_dealt(slot_factor, PACK, "os_col")
+        memq_col = load_dealt(memq, PARITIES, "memq_col")
+        nc.sync.dma_start(val_pool[3][:], vals_planes[3])
 
-        lam_col = sb.tile([P, HALVES], F32, name="lam_col", tag="lam_col", align_bytes=64)
-        nc.sync.dma_start(lam_col[:], lam.rearrange("o (p a) -> p (o a)", a=HALVES))
-        os_col = sb.tile([P, PACK], F32, name="os_col")
-        nc.sync.dma_start(os_col[:], slot_factor.rearrange("o (p m) -> p (o m)", m=PACK))
-        memq_col = sb.tile([P, HALVES], F32, name="memq_col")
-        nc.sync.dma_start(memq_col[:], memq.rearrange("o (p a) -> p (o a)", a=HALVES))
-        eager_col = sb.tile([P, HALVES], F32, name="eager_col")
-        nc.sync.dma_start(eager_col[:], eager.rearrange("(p a) o -> p (a o)", a=HALVES))
-        thresh_col = sb.tile([P, HALVES], F32, name="thresh_col")
-        nc.sync.dma_start(thresh_col[:], thresh.rearrange("(p a) o -> p (a o)", a=HALVES))
-        for t in range(1, PACK):
-            nc.sync.dma_start(val_pool[t][:], vals_planes[t])
-
-        ident = sb.tile([P, P], F32, name="ident")
+        ident = tile([P, P], F32, "ident")
         make_identity(nc, ident[:])
 
-        query_bf = sb.tile([P, Q, PACK], BF16, name="query_bf", tag="query_bf", align_bytes=64)
-        nc.scalar.activation(
-            query_bf[:].rearrange("p (c i) t -> p c t i", i=4),
-            query_raw[:].rearrange("p t (c i) -> p c t i", i=4),
-            ACT.Copy,
-        )
-        key_scales = sb.tile([P, I], U8, name="key_scales", align_bytes=64)
+        query_bf = tile([P, Q, PACK], BF16, "query_bf")
+        nc.scalar.activation(*weave_views(query_bf[:], query_raw[:]), ACT.Copy)
+        key_scales = tile([P, I], U8, "key_scales")
         nc.vector.tensor_copy(key_scales[:], key_scale_pool[:].indirect(offsets[:]))
-        half = I // 32
-        key_words = [sb.tile([P, I // 2], U16, name="key_words0", align_bytes=64)]
-        nc.vector.tensor_copy(key_words[0][:], key_word_pool[:].indirect(offsets[:, 0:half]))
-        query_codes = sb.tile([P, Q], U32, name="query_codes", align_bytes=64)
-        query_scales = sb.tile([P, Q], U8, name="query_scales", align_bytes=64)
-        nc.vector.quantize_mx(
-            out=query_codes[:].bitcast(FP8X4), scales=query_scales[:], in_=query_bf[:].rearrange("p q t -> p (q t)")
-        )
+        half_cols = LIST_COLS // 2
+        key_words = [tile([P, I // 2], U16, "key_words0")]
+        nc.vector.tensor_copy(key_words[0][:], key_word_pool[:].indirect(offsets[:, 0:half_cols]))
+        query_codes = tile([P, Q], U32, "query_codes")
+        query_scales = tile([P, Q], U8, "query_scales")
+        quantize(query_codes[:], query_scales[:], query_bf[:].rearrange("p q t -> p (q t)"))
+        key_words.append(tile([P, I // 2], U16, "key_words1", after="query_bf"))
+        nc.vector.tensor_copy(key_words[1][:], key_word_pool[:].indirect(offsets[:, half_cols:LIST_COLS]))
 
-        key_words.append(sb.tile([P, I // 2], U16, name="key_words1", tag="query_bf", align_bytes=64))
-        nc.vector.tensor_copy(key_words[1][:], key_word_pool[:].indirect(offsets[:, half : 2 * half]))
-        raw_ps = [bank([P, 2, Q], h, "raw_ps%d" % h) for h in range(2)]
-        for r in range(4):
-            cols = slice(r * P, (r + 1) * P)
+        a0_ps = [bank([P, Q], number, "a0_ps%d" % number) for number in (0, 1, 5, 7)]
+        for r in range(SLOT_TILES):
             nc.tensor.matmul_mx(
-                out=raw_ps[r // 2][:, r % 2, :],
+                out=a0_ps[r][:],
                 lhsT=key_words[r // 2][:, (r % 2) * P : (r % 2 + 1) * P].bitcast(FP4X4),
-                lhsT_scale=key_scales[:, cols],
+                lhsT_scale=key_scales[:, r * P : (r + 1) * P],
                 rhs=query_codes[:].bitcast(FP8X4),
                 rhs_scale=query_scales[:],
                 start=True,
                 stop=True,
             )
 
-        best = [sb.tile([P, 2 * V, 1], F32, name="best%d" % h) for h in range(2)]
-        best_rep = [sb.tile([P, 2 * V, P // V], F32, name="best_rep%d" % h) for h in range(2)]
-        raw_sb = [sb.tile([P, 2, HALVES, P], F32, name="raw_sb%d" % h) for h in range(2)]
-        for h in range(2):
+        best = [tile([P, 2 * V, 1], F32, "best%d" % h) for h in range(2)]
+        a0_sb = [tile([P, PARITIES, P], F32, "a0_sb%d" % r) for r in range(SLOT_TILES)]
+        for r in range(SLOT_TILES):
             nc.vector.tensor_reduce(
-                best[h][:, :, 0],
-                raw_ps[h][:].rearrange("p r (v j) -> p (r v) j", j=GROUP),
+                best[r // 2][:, (r % 2) * V : (r % 2 + 1) * V, 0],
+                a0_ps[r][:].rearrange("p (v j) -> p v j", j=GROUP),
                 AX.X,
                 ALU.max,
             )
-            nc.scalar.copy(raw_sb[h][:], raw_ps[h][:].rearrange("p r (m a) -> p r a m", a=HALVES))
+            nc.scalar.copy(a0_sb[r][:], a0_ps[r][:].rearrange("p (m a) -> p a m", a=PARITIES))
+        best_rep = [tile([P, 2 * V, P // V], F32, "best_rep%d" % h) for h in range(2)]
         for h in range(2):
             nc.vector.tensor_copy(best_rep[h][:], best[h][:].to_broadcast([P, 2 * V, P // V]))
-        best_t = sb.tile([P, I], F32, name="best_t", tag="best_t", align_bytes=64)
-        raw_t_ps = [bank([P, 4, P], 2 + a, "raw_t_ps%d" % a) for a in range(HALVES)]
+        best_t = tile([P, I], F32, "best_t")
         for h in range(2):
             best_ps = bank([P, 2, P], 4 + 2 * h, "best_ps%d" % h)
             for r in range(2):
                 nc.tensor.transpose(
                     best_ps[:, r, :], best_rep[h][:, V * r : V * (r + 1), :].rearrange("p v j -> p (v j)"), ident[:]
                 )
-            nc.scalar.copy(best_t[:, 2 * P * h : 2 * P * (h + 1)], best_ps[:].rearrange("p r m -> p (r m)"))
-        for a in range(HALVES):
-            for r in range(4):
-                nc.tensor.transpose(raw_t_ps[a][:, r, :], raw_sb[r // 2][:, r % 2, a, :], ident[:])
+            nc.scalar.copy(best_t[:, 2 * P * h : 2 * P * (h + 1)], best_ps[:].rearrange("p r s -> p (r s)"))
+        a0_t_ps = [bank([P, SLOT_TILES, P], 2 + a, "a0_t_ps%d" % a) for a in range(PARITIES)]
+        for a in range(PARITIES):
+            for r in range(SLOT_TILES):
+                nc.tensor.transpose(a0_t_ps[a][:, r, :], a0_sb[r][:, a, :], ident[:])
 
-        val_codes = [sb.tile([P, P], U32, name="val_codes%d" % t, align_bytes=64) for t in range(PACK)]
-        val_scales = [sb.tile([P, P], U8, name="val_scales%d" % t, align_bytes=64) for t in range(PACK)]
-        val_bf = []
-
-        def gather_vals(t):
-            picked = sb.tile([P, I], BF16, name="picked%d" % t, tag=("picked0", "best_t", "lam_col", "p1")[t], align_bytes=64)
+        def gather_on_vector(t, after=None):
+            picked = tile([P, I], BF16, "picked%d" % t, after)
             nc.vector.tensor_copy(picked[:], val_pool[t][:].indirect(offsets[:]))
-            pairs = picked[:].bitcast(F32)
-            turned = bank([P, 2, P], (6, 7, 6, 4)[t], "val_turned%d" % t)
-            for u in range(2):
-                nc.tensor.transpose(turned[:, u, :], pairs[:, u : 2 * P : 2], ident[:])
-            return turned
+            return picked
 
-        def weave_vals(t, turned):
-            val_bf.append(
-                sb.tile([P, P, PACK], BF16, name="val_bf%d" % t, tag=("val_bf0", "odds", "p_sum", "val_bf3")[t], align_bytes=64)
-            )
+        def weave_vals(turned, name, after=None):
+            woven = tile([P, 2 * P * PACK], BF16, name, after)
             nc.scalar.copy(
-                val_bf[t][:].rearrange("p e t -> p (e t)").bitcast(F32).rearrange("p (e u) -> p e u", u=2),
-                turned[:].rearrange("p u e -> p e u"),
+                woven[:].bitcast(F32).rearrange("p (k m u) -> p k m u", k=2, u=2),
+                turned[:].rearrange("p k u m -> p k m u"),
             )
+            return woven
 
-        def quantize_vals(t):
-            nc.vector.quantize_mx(
-                out=val_codes[t][:].bitcast(FP8X4), scales=val_scales[t][:], in_=val_bf[t][:].rearrange("p e t -> p (e t)")
-            )
+        def quantize_vals(woven, name, after=None):
+            codes = tile([P, 2 * P], U32, name + "_codes", after)
+            scales = tile([P, 2 * P], U8, name + "_scales")
+            quantize(codes[:], scales[:], woven[:])
+            return codes, scales
 
-        weave_vals(0, gather_vals(0))
+        val_pool_bf = tile([P, T], BF16, "val_pool_bf", after="best_rep1")
+        nc.scalar.activation(val_pool_bf[:], val_pool[SCALAR_PLANE][:], ACT.Copy)
+        low_turned = bank([P, 2, 2, P], 0, "low_turned")
+        turn_pairs(low_turned[:, 0, :, :], gather_on_vector(0)[:])
 
-        os_ps = bank([P, PACK, P], 5, "os_ps")
-        for m in range(PACK):
-            nc.tensor.transpose(os_ps[:, m, :], os_col[:, m : m + 1].to_broadcast([P, P]), ident[:])
-        memq_ps = bank([P, HALVES, P], 7, "memq_ps")
-        for a in range(HALVES):
-            nc.tensor.transpose(memq_ps[:, a, :], memq_col[:, a : a + 1].to_broadcast([P, P]), ident[:])
-        memq_row = sb.tile([P, 1, Q], F32, name="memq_row")
-        nc.scalar.copy(memq_row[:, 0, :].rearrange("p (m a) -> p m a", a=HALVES), memq_ps[:].rearrange("p a m -> p m a"))
+        os_ps = bank([P, PACK, P], 6, "os_ps")
+        for c in range(PACK):
+            nc.tensor.transpose(os_ps[:, c, :], os_col[:, c : c + 1].to_broadcast([P, P]), ident[:])
+        memq_ps = bank([P, PARITIES, P], 7, "memq_ps")
+        for c in range(PARITIES):
+            nc.tensor.transpose(memq_ps[:, c, :], memq_col[:, c : c + 1].to_broadcast([P, P]), ident[:])
 
-        neg_both = sb.tile([P, HALVES * I], F32, name="neg_both", tag="val_pool0", align_bytes=64)
-        neg_s = [neg_both[:, a * I : (a + 1) * I] for a in range(HALVES)]
-        neg_sum = sb.tile([P, HALVES], F32, name="neg_sum")
-        neg_max = sb.tile([P, HALVES], F32, name="neg_max")
-        gap = sb.tile([P, HALVES], F32, name="gap")
-        p_sum = sb.tile([P, HALVES], F32, name="p_sum", tag="p_sum", align_bytes=64)
-        odds = sb.tile([P, HALVES], F32, name="odds", tag="odds", align_bytes=64)
-        denom = sb.tile([P, HALVES], F32, name="denom")
-        p = [sb.tile([P, I], F32, name="p%d" % a, tag="p%d" % a, align_bytes=64) for a in range(HALVES)]
-        for a in range(HALVES):
+        neg_scores = tile([P, PARITIES, I], F32, "neg_scores", after="val_pool0")
+        exps = tile([P, PARITIES * I + PARITIES], F32, "exps", after="val_pool%d" % SCALAR_PLANE)
+        p = [exps[:, a * I : (a + 1) * I] for a in range(PARITIES)]
+        odds = exps[:, PARITIES * I : PARITIES * I + PARITIES]
+        neg_sum = tile([P, PARITIES], F32, "neg_sum")
+        neg_max = tile([P, PARITIES], F32, "neg_max")
+        p_sum = tile([P, PARITIES], F32, "p_sum")
+        for a in range(PARITIES):
             nc.vector.scalar_tensor_tensor(
-                neg_s[a], best_t[:], lam_col[:, a : a + 1], raw_t_ps[a][:].rearrange("p r m -> p (r m)"),
+                neg_scores[:, a, :], best_t[:], lam_col[:, a : a + 1], a0_t_ps[a][:].rearrange("p r s -> p (r s)"),
                 ALU.mult, ALU.subtract, accum_out=neg_sum[:, a : a + 1],
             )
-        for a in range(HALVES):
+        for a in range(PARITIES):
+            nc.vector.tensor_reduce(neg_max[:, a : a + 1], neg_scores[:, a, :], AX.X, ALU.min)
+            nc.scalar.activation(
+                p[a], neg_scores[:, a, :], ACT.Exp, bias=neg_max[:, a : a + 1], scale=-1.0, accum_out=p_sum[:, a : a + 1]
+            )
+        mean_less_max = tile([P, PARITIES], F32, "mean_less_max")
+        nc.vector.scalar_tensor_tensor(mean_less_max[:], neg_sum[:], -1.0 / I, neg_max[:], ALU.mult, ALU.add)
+        for a in range(PARITIES):
             col = slice(a, a + 1)
-            nc.vector.tensor_reduce(neg_max[:, col], neg_s[a], AX.X, ALU.min)
-            nc.scalar.activation(p[a][:], neg_s[a], ACT.Exp, bias=neg_max[:, col], scale=-1.0, accum_out=p_sum[:, col])
-            nc.gpsimd.tensor_scalar(gap[:, col], neg_sum[:, col], -1.0 / I, neg_max[:, col], ALU.mult, ALU.add)
-        for a in range(HALVES):
-            col = slice(a, a + 1)
-            nc.scalar.activation(odds[:, col], gap[:, col], ACT.Exp, bias=thresh_col[:, col], scale=eager_col[:, col])
-        for a in range(HALVES):
+            nc.scalar.activation(odds[:, col], mean_less_max[:, col], ACT.Exp, bias=thresh_col[:, col], scale=eager_col[:, col])
+        denom = tile([P, PARITIES], F32, "denom")
+        for a in range(PARITIES):
             col = slice(a, a + 1)
             nc.scalar.activation(denom[:, col], odds[:, col], ACT.Identity, bias=p_sum[:, col], scale=p_sum[:, col])
-        weave_vals(1, gather_vals(1))
-        quantize_vals(0)
-        weave_vals(2, gather_vals(2))
-        factor = sb.tile([P, HALVES], F32, name="factor", tag="val_pool2", align_bytes=64)
+
+        turn_pairs(low_turned[:, 1, :, :], gather_on_vector(1, after="neg_sum")[:])
+        picked_by_scalar = tile([P, I], BF16, "picked_by_scalar", after="p_sum")
+        nc.scalar.activation(picked_by_scalar[:], val_pool_bf[:].indirect(offsets[:]), ACT.Copy)
+        low_woven = weave_vals(low_turned, "low_woven", after="mean_less_max")
+        memq_row = tile([P, 1, Q], F32, "memq_row", after="best_rep1")
+        nc.scalar.copy(memq_row[:, 0, :].rearrange("p (n c) -> p n c", c=PARITIES), memq_ps[:].rearrange("p c n -> p n c"))
+        factor = tile([P, PARITIES], F32, "factor", after="val_pool1")
         nc.vector.reciprocal(factor[:], denom[:])
 
-        w_bf = [sb.tile([P, I], BF16, name="w_bf%d" % a, align_bytes=64) for a in range(HALVES)]
-        w_ps = bank([P, 2, HALVES, P], 4, "w_ps")
-        for a in range(HALVES):
+        w_ps = bank([P, 2, PARITIES, P], 4, "w_ps")
+        for a in range(PARITIES):
+            w_bf = tile([P, I], BF16, "w_bf%d" % a)
             nc.vector.scalar_tensor_tensor(
-                w_bf[a][:].rearrange("p (n m) -> p n m", m=PACK),
-                p[a][:].rearrange("p (n m) -> p n m", m=PACK),
+                w_bf[:].rearrange("p (n c) -> p n c", c=PACK),
+                p[a].rearrange("p (n c) -> p n c", c=PACK),
                 factor[:, a : a + 1],
-                os_ps[:].rearrange("p m n -> p n m"),
+                os_ps[:].rearrange("p c n -> p n c"),
                 ALU.mult, ALU.mult,
             )
-            pairs = w_bf[a][:].bitcast(F32)
-            for u in range(2):
-                nc.tensor.transpose(w_ps[:, u, a, :], pairs[:, u : 2 * P : 2], ident[:])
-        w_t = sb.tile([P, Q * PACK], BF16, name="w_t", align_bytes=64)
+            turn_pairs(w_ps[:, :, a, :], w_bf[:])
+        w_woven = tile([P, Q * PACK], BF16, "w_woven")
         nc.scalar.copy(
-            w_t[:].bitcast(F32).rearrange("p (m a u) -> p m a u", a=HALVES, u=2),
+            w_woven[:].bitcast(F32).rearrange("p (m a u) -> p m a u", a=PARITIES, u=2),
             w_ps[:].rearrange("p u a m -> p m a u"),
         )
-        quantize_vals(1)
-        weave_vals(3, gather_vals(3))
-        quantize_vals(2)
-        w_codes = sb.tile([P, Q], U32, name="w_codes", tag="val_pool3", align_bytes=64)
-        w_scales = sb.tile([P, Q], U8, name="w_scales", align_bytes=64)
-        nc.vector.quantize_mx(out=w_codes[:].bitcast(FP8X4), scales=w_scales[:], in_=w_t[:])
-        quantize_vals(3)
+        high_turned = bank([P, 2, 2, P], 6, "high_turned")
+        turn_pairs(high_turned[:, 0, :, :], picked_by_scalar[:])
+        turn_pairs(high_turned[:, 1, :, :], gather_on_vector(3, after="val_pool1")[:])
+        high_woven = weave_vals(high_turned, "high_woven")
+        low_vals = quantize_vals(low_woven, "low", after="val_pool%d" % SCALAR_PLANE)
+        w_codes = tile([P, Q], U32, "w_codes", after="val_pool3")
+        w_scales = tile([P, Q], U8, "w_scales")
+        quantize(w_codes[:], w_scales[:], w_woven[:])
 
-        o_ps = [bank([P, 2, Q], h, "o_ps%d" % h) for h in range(2)]
-        for t in range(PACK):
-            nc.tensor.matmul_mx(
-                out=o_ps[t // 2][:, t % 2, :],
-                lhsT=val_codes[t][:].bitcast(FP8X4),
-                lhsT_scale=val_scales[t][:],
-                rhs=w_codes[:].bitcast(FP8X4),
-                rhs_scale=w_scales[:],
-                start=True,
-                stop=True,
-            )
-        carried = [sb.tile([P, 2, Q], F32, name="carried%d" % h) for h in range(2)]
-        y = sb.tile([P, PACK, Q], F32, name="y")
-        out_rows = out_0.rearrange("(p t) q -> p t q", t=PACK)
-        for h in range(2):
-            nc.vector.memset(carried[h][:, :, 0:1], 0.0)
-        for h in range(2):
+        def product(val_operand, number):
+            codes, scales = val_operand
+            o_ps = bank([P, 2, Q], number, "o_ps%d" % number)
+            for k in range(2):
+                nc.tensor.matmul_mx(
+                    out=o_ps[:, k, :],
+                    lhsT=codes[:, k * P : (k + 1) * P].bitcast(FP8X4),
+                    lhsT_scale=scales[:, k * P : (k + 1) * P],
+                    rhs=w_codes[:].bitcast(FP8X4),
+                    rhs_scale=w_scales[:],
+                    start=True,
+                    stop=True,
+                )
+            return o_ps
+
+        def carry(carried, o_ps, first, last):
             nc.vector.tensor_tensor(
-                carried[h][:, :, 1:Q], o_ps[h][:, :, 0 : Q - 1],
-                memq_row[:, :, 1:Q].to_broadcast([P, 2, Q - 1]), ALU.mult,
+                carried[:, :, first:last], o_ps[:, :, first - 1 : last - 1],
+                memq_row[:, :, first:last].to_broadcast([P, 2, last - first]), ALU.mult,
             )
-        for h in range(2):
-            nc.vector.tensor_tensor(y[:, 2 * h : 2 * h + 2, :], o_ps[h][:], carried[h][:], ALU.subtract)
-            nc.sync.dma_start(out_rows[:, 2 * h : 2 * h + 2, :], y[:, 2 * h : 2 * h + 2, :])
 
-        y_codes = sb.tile([P, Q], U32, name="y_codes", align_bytes=64)
-        y_scales = sb.tile([P, Q], U8, name="y_scales", align_bytes=64)
-        y_bf = sb.tile([P, Q, PACK], BF16, name="y_bf", align_bytes=64)
-        nc.vector.tensor_copy(
-            y_bf[:].rearrange("p (c i) t -> p c t i", i=4), y[:].rearrange("p t (c i) -> p c t i", i=4)
-        )
-        nc.vector.quantize_mx(
-            out=y_codes[:].bitcast(FP8X4), scales=y_scales[:], in_=y_bf[:].rearrange("p q t -> p (q t)")
-        )
+        low_carried = tile([P, 2, Q], F32, "low_carried")
+        high_carried = tile([P, 2, Q], F32, "high_carried")
+        for carried in (low_carried, high_carried):
+            nc.vector.memset(carried[:, :, 0:1], 0.0)
+        out_rows = out_0.rearrange("(m t) q -> m t q", t=PACK)
+
+        low_o = product(low_vals, 2)
+        carry(low_carried, low_o, 1, Q)
+        high_vals = quantize_vals(high_woven, "high")
+        y = tile([P, PACK, Q], F32, "y", after="high_woven")
+        nc.vector.tensor_tensor(y[:, 0:2, :], low_o[:], low_carried[:], ALU.subtract)
+        nc.sync.dma_start(out_rows[:, 0:2, :], y[:, 0:2, :])
+        high_o = product(high_vals, 3)
+        halves = [slice(0, Q // 2), slice(Q // 2, Q)]
+        for rows in halves:
+            carry(high_carried, high_o, max(rows.start, 1), rows.stop)
+        for rows in halves:
+            nc.vector.tensor_tensor(y[:, 2:4, rows], high_o[:, :, rows], high_carried[:, :, rows], ALU.subtract)
+        nc.sync.dma_start(out_rows[:, 2:4, :], y[:, 2:4, :])
+
+        y_woven = [tile([P, Q // 2, PACK], BF16, "y_woven%d" % c) for c in range(2)]
+        nc.scalar.copy(*weave_views(y_woven[0][:], y[:, :, halves[0]]))
+        nc.vector.tensor_copy(*weave_views(y_woven[1][:], y[:, :, halves[1]]))
+        y_codes = tile([P, Q], U32, "y_codes")
+        y_scales = tile([P, Q], U8, "y_scales")
+        for c, rows in enumerate(halves):
+            quantize(y_codes[:, rows], y_scales[:, rows], y_woven[c][:].rearrange("p q t -> p (q t)"))
         nc.sync.dma_start(out_1[0].rearrange("p c r -> p (c r)").bitcast(I32), y_codes[:].bitcast(I32))
-        for quad in range(4):
+        for quad in range(QUADS):
             queue = nc.scalar if quad % 2 == 0 else nc.sync
             queue.dma_start(
                 out_2[0, 4 * quad : 4 * quad + 4, :].bitcast(I32),

@@ -79,10 +79,10 @@ def tile_attend_groupbest_abstaining_rowchanges_pl_kernel(
         nc.sync.dma_start(val_pool[0][:], vals_planes[0])
         lam_col = load_dealt(lam, PARITIES, "lam_col")
         nc.sync.dma_start(val_pool[SCALAR_PLANE][:], vals_planes[SCALAR_PLANE])
+        os_col = load_dealt(slot_factor, PACK, "os_col")
         nc.sync.dma_start(val_pool[1][:], vals_planes[1])
         eager_col = load_dealt(eager, PARITIES, "eager_col")
         thresh_col = load_dealt(thresh, PARITIES, "thresh_col")
-        os_col = load_dealt(slot_factor, PACK, "os_col")
         memq_col = load_dealt(memq, PARITIES, "memq_col")
         nc.sync.dma_start(val_pool[3][:], vals_planes[3])
 
@@ -145,13 +145,11 @@ def tile_attend_groupbest_abstaining_rowchanges_pl_kernel(
             nc.vector.tensor_copy(picked[:], val_pool[t][:].indirect(offsets[:]))
             return picked
 
-        def weave_vals(turned, name, after=None):
-            woven = tile([P, 2 * P * PACK], BF16, name, after)
+        def weave_vals(woven, turned):
             nc.scalar.copy(
-                woven[:].bitcast(F32).rearrange("p (k m u) -> p k m u", k=2, u=2),
-                turned[:].rearrange("p k u m -> p k m u"),
+                woven.bitcast(F32).rearrange("p (k m u) -> p k m u", m=P, u=2),
+                turned.rearrange("p k u m -> p k m u"),
             )
-            return woven
 
         def quantize_vals(woven, name, after=None):
             codes = tile([P, 2 * P], U32, name + "_codes", after)
@@ -201,11 +199,12 @@ def tile_attend_groupbest_abstaining_rowchanges_pl_kernel(
         turn_pairs(low_turned[:, 1, :, :], gather_on_vector(1, after="neg_sum")[:])
         picked_by_scalar = tile([P, I], BF16, "picked_by_scalar", after="p_sum")
         nc.scalar.activation(picked_by_scalar[:], val_pool_bf[:].indirect(offsets[:]), ACT.Copy)
-        low_woven = weave_vals(low_turned, "low_woven", after="mean_less_max")
-        memq_row = tile([P, 1, Q], F32, "memq_row", after="best_rep1")
-        nc.scalar.copy(memq_row[:, 0, :].rearrange("p (n c) -> p n c", c=PARITIES), memq_ps[:].rearrange("p c n -> p n c"))
         factor = tile([P, PARITIES], F32, "factor", after="val_pool1")
         nc.vector.reciprocal(factor[:], denom[:])
+        low_woven = tile([P, 2 * P * PACK], BF16, "low_woven", after="denom")
+        weave_vals(low_woven[:], low_turned[:])
+        memq_row = tile([P, 1, Q], F32, "memq_row", after="best_rep1")
+        nc.scalar.copy(memq_row[:, 0, :].rearrange("p (n c) -> p n c", c=PARITIES), memq_ps[:].rearrange("p c n -> p n c"))
 
         w_ps = bank([P, 2, PARITIES, P], 4, "w_ps")
         for a in range(PARITIES):
@@ -223,10 +222,11 @@ def tile_attend_groupbest_abstaining_rowchanges_pl_kernel(
             w_woven[:].bitcast(F32).rearrange("p (m a u) -> p m a u", a=PARITIES, u=2),
             w_ps[:].rearrange("p u a m -> p m a u"),
         )
-        high_turned = bank([P, 2, 2, P], 6, "high_turned")
-        turn_pairs(high_turned[:, 0, :, :], picked_by_scalar[:])
-        turn_pairs(high_turned[:, 1, :, :], gather_on_vector(3, after="val_pool1")[:])
-        high_woven = weave_vals(high_turned, "high_woven")
+        high_woven = tile([P, 2 * P * PACK], BF16, "high_woven")
+        for k, (number, picked) in enumerate(((6, picked_by_scalar), (1, gather_on_vector(3, after="val_pool1")))):
+            turned = bank([P, 1, 2, P], number, "high_turned%d" % k)
+            turn_pairs(turned[:, 0, :, :], picked[:])
+            weave_vals(high_woven[:, k * P * PACK : (k + 1) * P * PACK], turned[:])
         low_vals = quantize_vals(low_woven, "low", after="val_pool%d" % SCALAR_PLANE)
         w_codes = tile([P, Q], U32, "w_codes", after="val_pool3")
         w_scales = tile([P, Q], U8, "w_scales")
@@ -247,31 +247,29 @@ def tile_attend_groupbest_abstaining_rowchanges_pl_kernel(
                 )
             return o_ps
 
-        def carry(carried, o_ps, first, last):
+        def carry(dest, o_ps, first, last):
             nc.vector.tensor_tensor(
-                carried[:, :, first:last], o_ps[:, :, first - 1 : last - 1],
+                dest[:, :, first:last], o_ps[:, :, first - 1 : last - 1],
                 memq_row[:, :, first:last].to_broadcast([P, 2, last - first]), ALU.mult,
             )
 
-        low_carried = tile([P, 2, Q], F32, "low_carried")
-        high_carried = tile([P, 2, Q], F32, "high_carried")
-        for carried in (low_carried, high_carried):
-            nc.vector.memset(carried[:, :, 0:1], 0.0)
-        out_rows = out_0.rearrange("(m t) q -> m t q", t=PACK)
-
         low_o = product(low_vals, 2)
-        carry(low_carried, low_o, 1, Q)
         high_vals = quantize_vals(high_woven, "high")
-        y = tile([P, PACK, Q], F32, "y", after="high_woven")
-        nc.vector.tensor_tensor(y[:, 0:2, :], low_o[:], low_carried[:], ALU.subtract)
-        nc.sync.dma_start(out_rows[:, 0:2, :], y[:, 0:2, :])
         high_o = product(high_vals, 3)
+        carried = tile([P, PACK, Q], F32, "carried", after="high_woven")
+        nc.vector.memset(carried[:, :, 0:1], 0.0)
+        y = tile([P, PACK, Q], F32, "y")
+        out_rows = out_0.rearrange("(m t) q -> m t q", t=PACK)
+        low, high = slice(0, 2), slice(2, 4)
+        carry(carried[:, low, :], low_o, 1, Q)
+        nc.vector.tensor_tensor(y[:, low, :], low_o[:], carried[:, low, :], ALU.subtract)
+        nc.sync.dma_start(out_rows[:, low, :], y[:, low, :])
         halves = [slice(0, Q // 2), slice(Q // 2, Q)]
         for rows in halves:
-            carry(high_carried, high_o, max(rows.start, 1), rows.stop)
+            carry(carried[:, high, :], high_o, max(rows.start, 1), rows.stop)
         for rows in halves:
-            nc.vector.tensor_tensor(y[:, 2:4, rows], high_o[:, :, rows], high_carried[:, :, rows], ALU.subtract)
-        nc.sync.dma_start(out_rows[:, 2:4, :], y[:, 2:4, :])
+            nc.vector.tensor_tensor(y[:, high, rows], high_o[:, :, rows], carried[:, high, rows], ALU.subtract)
+        nc.sync.dma_start(out_rows[:, high, :], y[:, high, :])
 
         y_woven = [tile([P, Q // 2, PACK], BF16, "y_woven%d" % c) for c in range(2)]
         nc.scalar.copy(*weave_views(y_woven[0][:], y[:, :, halves[0]]))

from contextlib import ExitStack

import concourse.mybir as mybir
from concourse.masks import make_identity

D, T, I, Q, E, V = 512, 2048, 512, 256, 512, 32
FLOPS = 2 * D * I * Q + 2 * I * E * Q

F32 = mybir.dt.float32
BF16 = mybir.dt.bfloat16
I32 = mybir.dt.int32
U32 = mybir.dt.uint32
U16 = mybir.dt.uint16
U8 = mybir.dt.uint8
FP8X4 = mybir.dt.float8_e4m3fn_x4
FP4X4 = mybir.dt.float4_e2m1fn_x4
ALU = mybir.AluOpType
ACT = mybir.ActivationFunctionType
AX = mybir.AxisListType

P = 128
PACK = 4
QUADS = 4
GROUP = Q // V
PARITIES = Q // P
SLOT_TILES = I // P
LIST_COLS = I // 16
SCALAR_PLANE = 2
RUN = 4


def tile_attend_groupbest_abstaining_rowchanges_pl_kernel(
    tc, query, keys_words, keys_scales, lam, eager, thresh, slot_factor, vals, memq, offs, out_0, out_1, out_2
):
    nc = tc.nc
    with ExitStack() as ctx:
        sb = ctx.enter_context(tc.tile_pool(name="sb", bufs=1))
        ps = ctx.enter_context(tc.psum_pool(name="ps", bufs=1))

        def tile(shape, dtype, name, after=None):
            return sb.tile(shape, dtype, name=name, tag=after or name, align_bytes=64)

        def bank(shape, number, name):
            return ps.tile(shape, F32, name=name, tag="bank%d" % number)

        def load_dealt(vector, width, name):
            pattern = "o (m c) -> m (o c)" if vector.shape[0] == 1 else "(m c) o -> m (c o)"
            col = tile([P, width], F32, name)
            nc.sync.dma_start(col[:], vector.rearrange(pattern, c=width))
            return col

        def weave_views(woven, rows):
            return woven.rearrange("p (c i) t -> p c t i", i=RUN), rows.rearrange("p t (c i) -> p c t i", i=RUN)

        def quantize(codes, scales, woven):
            nc.vector.quantize_mx(out=codes.bitcast(FP8X4), scales=scales, in_=woven)

        def turn_pairs(turned, values):
            pairs = values.bitcast(F32)
            for u in range(2):
                nc.tensor.transpose(turned[:, u, :], pairs[:, u : I // 2 : 2], ident[:])

        offsets = sb.tile([P, LIST_COLS], U16, name="offsets")
        nc.sync.dma_start(offsets[:], offs)
        key_scale_pool = tile([P, T], U8, "key_scale_pool")
        nc.vector.memset(key_scale_pool[:].bitcast(I32), 0)
        query_raw = tile([P, PACK, Q], F32, "query_raw")
        nc.sync.dma_start(query_raw[:], query.rearrange("(p t) q -> p t q", t=PACK))
        for quad in range(QUADS):
            nc.sync.dma_start(
                key_scale_pool[32 * quad : 32 * quad + 4, :].bitcast(I32),
                keys_scales[0, 4 * quad : 4 * quad + 4, :].bitcast(I32),
            )
        key_word_pool = tile([P, T], U16, "key_word_pool")
        nc.sync.dma_start(key_word_pool[:].bitcast(I32), keys_words[0].bitcast(I32))

        vals_planes = vals.rearrange("(m t) c -> t m c", t=PACK)
        val_pool = [tile([P, T], F32, "val_pool%d" % t) for t in range(PACK)]
        nc.sync.dma_start(val_pool[0][:], vals_planes[0])
        lam_col = load_dealt(lam, PARITIES, "lam_col")
        nc.sync.dma_start(val_pool[SCALAR_PLANE][:], vals_planes[SCALAR_PLANE])
        os_col = load_dealt(slot_factor, PACK, "os_col")
        nc.sync.dma_start(val_pool[1][:], vals_planes[1])
        eager_col = load_dealt(eager, PARITIES, "eager_col")
        thresh_col = load_dealt(thresh, PARITIES, "thresh_col")
        memq_col = load_dealt(memq, PARITIES, "memq_col")
        nc.sync.dma_start(val_pool[3][:], vals_planes[3])

        ident = tile([P, P], F32, "ident")
        make_identity(nc, ident[:])

        query_bf = tile([P, Q, PACK], BF16, "query_bf")
        nc.scalar.activation(*weave_views(query_bf[:], query_raw[:]), ACT.Copy)
        key_scales = tile([P, I], U8, "key_scales")
        nc.vector.tensor_copy(key_scales[:], key_scale_pool[:].indirect(offsets[:]))
        half_cols = LIST_COLS // 2
        key_words = [tile([P, I // 2], U16, "key_words0")]
        nc.vector.tensor_copy(key_words[0][:], key_word_pool[:].indirect(offsets[:, 0:half_cols]))
        query_codes = tile([P, Q], U32, "query_codes")
        query_scales = tile([P, Q], U8, "query_scales")
        quantize(query_codes[:], query_scales[:], query_bf[:].rearrange("p q t -> p (q t)"))
        key_words.append(tile([P, I // 2], U16, "key_words1", after="query_bf"))
        nc.vector.tensor_copy(key_words[1][:], key_word_pool[:].indirect(offsets[:, half_cols:LIST_COLS]))

        a0_ps = [bank([P, Q], number, "a0_ps%d" % number) for number in (0, 1, 5, 7)]
        for r in range(SLOT_TILES):
            nc.tensor.matmul_mx(
                out=a0_ps[r][:],
                lhsT=key_words[r // 2][:, (r % 2) * P : (r % 2 + 1) * P].bitcast(FP4X4),
                lhsT_scale=key_scales[:, r * P : (r + 1) * P],
                rhs=query_codes[:].bitcast(FP8X4),
                rhs_scale=query_scales[:],
                start=True,
                stop=True,
            )

        best = [tile([P, 2 * V, 1], F32, "best%d" % h) for h in range(2)]
        a0_sb = [tile([P, PARITIES, P], F32, "a0_sb%d" % r) for r in range(SLOT_TILES)]
        for r in range(SLOT_TILES):
            nc.vector.tensor_reduce(
                best[r // 2][:, (r % 2) * V : (r % 2 + 1) * V, 0],
                a0_ps[r][:].rearrange("p (v j) -> p v j", j=GROUP),
                AX.X,
                ALU.max,
            )
            nc.scalar.copy(a0_sb[r][:], a0_ps[r][:].rearrange("p (m a) -> p a m", a=PARITIES))
        best_rep = [tile([P, 2 * V, P // V], F32, "best_rep%d" % h) for h in range(2)]
        for h in range(2):
            nc.vector.tensor_copy(best_rep[h][:], best[h][:].to_broadcast([P, 2 * V, P // V]))
        best_t = tile([P, I], F32, "best_t")
        for h in range(2):
            best_ps = bank([P, 2, P], 4 + 2 * h, "best_ps%d" % h)
            for r in range(2):
                nc.tensor.transpose(
                    best_ps[:, r, :], best_rep[h][:, V * r : V * (r + 1), :].rearrange("p v j -> p (v j)"), ident[:]
                )
            nc.scalar.copy(best_t[:, 2 * P * h : 2 * P * (h + 1)], best_ps[:].rearrange("p r s -> p (r s)"))
        a0_t_ps = [bank([P, SLOT_TILES, P], 2 + a, "a0_t_ps%d" % a) for a in range(PARITIES)]
        for a in range(PARITIES):
            for r in range(SLOT_TILES):
                nc.tensor.transpose(a0_t_ps[a][:, r, :], a0_sb[r][:, a, :], ident[:])

        def gather_on_vector(t, after=None):
            picked = tile([P, I], BF16, "picked%d" % t, after)
            nc.vector.tensor_copy(picked[:], val_pool[t][:].indirect(offsets[:]))
            return picked

        def weave_vals(woven, turned):
            nc.scalar.copy(
                woven.bitcast(F32).rearrange("p (k m u) -> p k m u", m=P, u=2),
                turned.rearrange("p k u m -> p k m u"),
            )

        def quantize_vals(woven, name, after=None):
            codes = tile([P, 2 * P], U32, name + "_codes", after)
            scales = tile([P, 2 * P], U8, name + "_scales")
            quantize(codes[:], scales[:], woven[:])
            return codes, scales

        val_pool_bf = tile([P, T], BF16, "val_pool_bf", after="best_rep1")
        nc.scalar.activation(val_pool_bf[:], val_pool[SCALAR_PLANE][:], ACT.Copy)
        low_turned = bank([P, 2, 2, P], 0, "low_turned")
        turn_pairs(low_turned[:, 0, :, :], gather_on_vector(0)[:])

        os_ps = bank([P, PACK, P], 6, "os_ps")
        for c in range(PACK):
            nc.tensor.transpose(os_ps[:, c, :], os_col[:, c : c + 1].to_broadcast([P, P]), ident[:])
        memq_ps = bank([P, PARITIES, P], 7, "memq_ps")
        for c in range(PARITIES):
            nc.tensor.transpose(memq_ps[:, c, :], memq_col[:, c : c + 1].to_broadcast([P, P]), ident[:])

        neg_scores = tile([P, PARITIES, I], F32, "neg_scores", after="val_pool0")
        exps = tile([P, PARITIES * I + PARITIES], F32, "exps", after="val_pool%d" % SCALAR_PLANE)
        p = [exps[:, a * I : (a + 1) * I] for a in range(PARITIES)]
        odds = exps[:, PARITIES * I : PARITIES * I + PARITIES]
        neg_sum = tile([P, PARITIES], F32, "neg_sum")
        neg_max = tile([P, PARITIES], F32, "neg_max")
        p_sum = tile([P, PARITIES], F32, "p_sum")
        for a in range(PARITIES):
            nc.vector.scalar_tensor_tensor(
                neg_scores[:, a, :], best_t[:], lam_col[:, a : a + 1], a0_t_ps[a][:].rearrange("p r s -> p (r s)"),
                ALU.mult, ALU.subtract, accum_out=neg_sum[:, a : a + 1],
            )
        for a in range(PARITIES):
            nc.vector.tensor_reduce(neg_max[:, a : a + 1], neg_scores[:, a, :], AX.X, ALU.min)
            nc.scalar.activation(
                p[a], neg_scores[:, a, :], ACT.Exp, bias=neg_max[:, a : a + 1], scale=-1.0, accum_out=p_sum[:, a : a + 1]
            )
        mean_less_max = tile([P, PARITIES], F32, "mean_less_max")
        nc.vector.scalar_tensor_tensor(mean_less_max[:], neg_sum[:], -1.0 / I, neg_max[:], ALU.mult, ALU.add)
        for a in range(PARITIES):
            col = slice(a, a + 1)
            nc.scalar.activation(odds[:, col], mean_less_max[:, col], ACT.Exp, bias=thresh_col[:, col], scale=eager_col[:, col])
        denom = tile([P, PARITIES], F32, "denom")
        for a in range(PARITIES):
            col = slice(a, a + 1)
            nc.scalar.activation(denom[:, col], odds[:, col], ACT.Identity, bias=p_sum[:, col], scale=p_sum[:, col])

        turn_pairs(low_turned[:, 1, :, :], gather_on_vector(1, after="neg_sum")[:])
        picked_by_scalar = tile([P, I], BF16, "picked_by_scalar", after="p_sum")
        nc.scalar.activation(picked_by_scalar[:], val_pool_bf[:].indirect(offsets[:]), ACT.Copy)
        factor = tile([P, PARITIES], F32, "factor", after="val_pool1")
        nc.vector.reciprocal(factor[:], denom[:])
        low_woven = tile([P, 2 * P * PACK], BF16, "low_woven", after="denom")
        weave_vals(low_woven[:], low_turned[:])
        memq_row = tile([P, 1, Q], F32, "memq_row", after="best_rep1")
        nc.scalar.copy(memq_row[:, 0, :].rearrange("p (n c) -> p n c", c=PARITIES), memq_ps[:].rearrange("p c n -> p n c"))

        w_ps = bank([P, 2, PARITIES, P], 4, "w_ps")
        for a in range(PARITIES):
            w_bf = tile([P, I], BF16, "w_bf%d" % a)
            nc.vector.scalar_tensor_tensor(
                w_bf[:].rearrange("p (n c) -> p n c", c=PACK),
                p[a].rearrange("p (n c) -> p n c", c=PACK),
                factor[:, a : a + 1],
                os_ps[:].rearrange("p c n -> p n c"),
                ALU.mult, ALU.mult,
            )
            turn_pairs(w_ps[:, :, a, :], w_bf[:])
        w_woven = tile([P, Q * PACK], BF16, "w_woven")
        nc.scalar.copy(
            w_woven[:].bitcast(F32).rearrange("p (m a u) -> p m a u", a=PARITIES, u=2),
            w_ps[:].rearrange("p u a m -> p m a u"),
        )
        high_woven = tile([P, 2 * P * PACK], BF16, "high_woven")
        for k, (number, picked) in enumerate(((6, picked_by_scalar), (1, gather_on_vector(3, after="val_pool1")))):
            turned = bank([P, 1, 2, P], number, "high_turned%d" % k)
            turn_pairs(turned[:, 0, :, :], picked[:])
            weave_vals(high_woven[:, k * P * PACK : (k + 1) * P * PACK], turned[:])
        low_vals = quantize_vals(low_woven, "low", after="val_pool%d" % SCALAR_PLANE)
        w_codes = tile([P, Q], U32, "w_codes", after="val_pool3")
        w_scales = tile([P, Q], U8, "w_scales")
        quantize(w_codes[:], w_scales[:], w_woven[:])

        def product(val_operand, number):
            codes, scales = val_operand
            o_ps = bank([P, 2, Q], number, "o_ps%d" % number)
            for k in range(2):
                nc.tensor.matmul_mx(
                    out=o_ps[:, k, :],
                    lhsT=codes[:, k * P : (k + 1) * P].bitcast(FP8X4),
                    lhsT_scale=scales[:, k * P : (k + 1) * P],
                    rhs=w_codes[:].bitcast(FP8X4),
                    rhs_scale=w_scales[:],
                    start=True,
                    stop=True,
                )
            return o_ps

        def carry(dest, o_ps, first, last):
            nc.vector.tensor_tensor(
                dest[:, :, first:last], o_ps[:, :, first - 1 : last - 1],
                memq_row[:, :, first:last].to_broadcast([P, 2, last - first]), ALU.mult,
            )

        low_o = product(low_vals, 2)
        high_vals = quantize_vals(high_woven, "high")
        high_o = product(high_vals, 3)
        carried = tile([P, PACK, Q], F32, "carried", after="high_woven")
        nc.vector.memset(carried[:, :, 0:1], 0.0)
        y = tile([P, PACK, Q], F32, "y")
        out_rows = out_0.rearrange("(m t) q -> m t q", t=PACK)
        low, high = slice(0, 2), slice(2, 4)
        carry(carried[:, low, :], low_o, 1, Q)
        nc.vector.tensor_tensor(y[:, low, :], low_o[:], carried[:, low, :], ALU.subtract)
        nc.sync.dma_start(out_rows[:, low, :], y[:, low, :])
        halves = [slice(0, Q // 2), slice(Q // 2, Q)]
        for rows in halves:
            carry(carried[:, high, :], high_o, max(rows.start, 1), rows.stop)
        for rows in halves:
            nc.vector.tensor_tensor(y[:, high, rows], high_o[:, :, rows], carried[:, high, rows], ALU.subtract)
        nc.sync.dma_start(out_rows[:, high, :], y[:, high, :])

        y_woven = [tile([P, Q // 2, PACK], BF16, "y_woven%d" % c) for c in range(2)]
        nc.scalar.copy(*weave_views(y_woven[0][:], y[:, :, halves[0]]))
        nc.vector.tensor_copy(*weave_views(y_woven[1][:], y[:, :, halves[1]]))
        y_codes = tile([P, Q], U32, "y_codes")
        y_scales = tile([P, Q], U8, "y_scales")
        for c, rows in enumerate(halves):
            quantize(y_codes[:, rows], y_scales[:, rows], y_woven[c][:].rearrange("p q t -> p (q t)"))
        nc.sync.dma_start(out_1[0].rearrange("p c r -> p (c r)").bitcast(I32), y_codes[:].bitcast(I32))
        for quad in range(QUADS):
            queue = nc.scalar if quad % 2 == 0 else nc.sync
            queue.dma_start(
                out_2[0, 4 * quad : 4 * quad + 4, :].bitcast(I32),
                y_scales[32 * quad : 32 * quad + 4, :].bitcast(I32),
            )
